import numpy as np
import ml_dtypes


def mxq(x, axis, fmt="e4m3"):
    dtype, down = {"e4m3": (ml_dtypes.float8_e4m3fn, 7), "e5m2": (ml_dtypes.float8_e5m2, 14)}[fmt]
    v = np.moveaxis(np.asarray(x, np.float32).astype(ml_dtypes.bfloat16).astype(np.float64), axis, -1)
    blocks = v.reshape(v.shape[:-1] + (-1, 32))
    amax = np.abs(blocks).max(-1, keepdims=True)
    byte = np.maximum(np.where(amax > 0, np.frexp(amax)[1] - 1 + 127, 0) - down, 1)
    scale = np.exp2(byte - 127.0)
    codes = (blocks / scale).astype(np.float32).astype(dtype).astype(np.float64)
    return np.moveaxis((codes * scale).reshape(v.shape), -1, axis)


WIDE = False


def mx_kscale(k):
    if not WIDE:
        return np.ones(k)
    levels = np.array([10, -10, 5, -5, 0])
    if k % 512:
        return np.exp2(np.random.permutation(np.resize(levels, k // 32))).repeat(32)
    a = np.empty((k // 512, 16))
    for p in range(k // 512):
        a[p, :8] = np.random.permutation(np.resize(levels, 8))
        for g in range(8):
            far = levels[np.abs(levels - a[p, g]) >= 10]
            a[p, g + 8] = far[np.random.randint(len(far))]
    return np.exp2(a.ravel()).repeat(32)


def f64(x):
    return np.asarray(x).astype(np.float64)


E2M1 = np.array([0.0, 0.5, 1.0, 1.5, 2.0, 3.0, 4.0, 6.0, -0.0, -0.5, -1.0, -1.5, -2.0, -3.0, -4.0, -6.0])


def pack_weight(w, fmt):
    k, n = w.shape
    w = f64(np.asarray(w, np.float32).astype(ml_dtypes.bfloat16)).reshape(k // 32, 32, n)
    amax = np.abs(w).max(1)
    if fmt == "e4m3":
        byte = np.frexp(amax)[1] - 1 + 127 - 7
    else:
        mant, ex = np.frexp(amax / 6.0)
        byte = np.where(mant > 0.5, ex, ex - 1) + 127
    byte = np.clip(np.where(amax > 0, byte, 1), 1, 254)
    scaled = (w * np.exp2(127.0 - byte)[:, None, :]).reshape(k, n).astype(np.float32)
    by_word = np.ascontiguousarray(scaled.reshape(k // 512, 128, 4, n).transpose(0, 1, 3, 2))
    if fmt == "e4m3":
        words = by_word.astype(ml_dtypes.float8_e4m3fn).view(np.uint8)
    else:
        c = by_word.astype(ml_dtypes.float4_e2m1fn).view(np.uint8) & 0xF
        words = (c[..., 0::2] | (c[..., 1::2] << 4)).reshape(k // 512, 128, 2 * n)
    return np.ascontiguousarray(words), np.ascontiguousarray(byte.astype(np.uint8).reshape(k // 512, 16, n))


def unpack_weight(words, scales, fmt):
    g, _, n = scales.shape
    words = np.ascontiguousarray(words).reshape(g, 128, n, -1)
    if fmt == "e4m3":
        vals = words.view(ml_dtypes.float8_e4m3fn).astype(np.float64)
    else:
        nib = np.empty((g, 128, n, 4), np.uint8)
        nib[..., 0::2] = words & 0xF
        nib[..., 1::2] = words >> 4
        vals = E2M1[nib]
    vals = vals * np.repeat(np.exp2(scales.astype(np.float64) - 127.0), 8, axis=1)[..., None]
    return vals.transpose(0, 1, 3, 2).reshape(g * 512, n)


def planes(y):
    n, m = y.shape
    v = y.astype(np.float32).astype(ml_dtypes.bfloat16).astype(np.float64).reshape(n // 32, 32, m)
    top = np.abs(v).max(1)
    byte = np.clip(np.where(top > 0, np.frexp(top)[1] - 1 + 127 - 7, 1), 1, 254)
    codes = (v * np.exp2(127.0 - byte)[:, None, :]).reshape(n, m).astype(np.float32).astype(ml_dtypes.float8_e4m3fn).view(np.uint8)
    words = codes.reshape(n // 512, 128, 4, m).transpose(0, 1, 3, 2)
    return np.ascontiguousarray(words), np.ascontiguousarray(byte.astype(np.uint8).reshape(n // 512, 16, m))


def silu(v):
    return v / (1.0 + np.exp(-np.maximum(v, -700.0)))


K, M, T = 512, 1024, 1536


def setup_inputs():
    n = np.random.standard_normal
    s = mx_kscale(K)[:, None]
    p_w4 = pack_weight(n((K, M)) / np.sqrt(K) / s, "e2m1")
    p_w8 = pack_weight(n((K, M)) / np.sqrt(K) / s, "e4m3")
    return {
        "x": (n((K, T)) * s).astype(np.float32),
        "w4_words": p_w4[0],
        "w4_scales": p_w4[1],
        "w8_words": p_w8[0],
        "w8_scales": p_w8[1],
    }


def reference(x, w4_words, w4_scales, w8_words, w8_scales):
    x_ = mxq(f64(x), 0, "e4m3")
    w4_ = unpack_weight(w4_words, w4_scales, "e2m1")
    w8_ = unpack_weight(w8_words, w8_scales, "e4m3")
    y = w4_.T @ x_
    u = w8_.T @ x_
    y = silu(y) * u
    out_0 = y
    return (out_0,) + planes(out_0)

@@ -1,0 +1,205 @@
+from contextlib import ExitStack
+
+import concourse.mybir as mybir
+
+K, M, T = 512, 1024, 1536
+FLOPS = 2 * 2 * K * M * T
+
+F32 = mybir.dt.float32
+BF16 = mybir.dt.bfloat16
+I32 = mybir.dt.int32
+U32 = mybir.dt.uint32
+U16 = mybir.dt.uint16
+U8 = mybir.dt.uint8
+FP8X4 = mybir.dt.float8_e4m3fn_x4
+FP4X4 = mybir.dt.float4_e2m1fn_x4
+SILU = mybir.ActivationFunctionType.Silu
+MULT = mybir.AluOpType.mult
+
+P = 128
+PACK = 4
+GROUP = P * PACK
+QUAD = 32
+W8_ROW = 4
+
+X_CHUNKS = [(0, 256), (256, 256), (512, 512), (1024, 512)]
+UNITS = [(0, 0, 256), (0, 256, 256), (1, 0, 512), (0, 512, 512), (1, 512, 512), (0, 1024, 512), (1, 1024, 256), (1, 1280, 256)]
+
+
+def deal(copy, dst, src, run):
+    copy(out=dst.rearrange("p (r c i) -> p c r i", r=PACK, i=run), in_=src.rearrange("p (c i r) -> p c r i", r=PACK, i=run))
+
+
+def round_columns(copy, dst, src, lo, hi):
+    copy(
+        out=dst[:, lo:hi, :].rearrange("p (c i) j -> p c j i", i=4),
+        in_=src[:, :, lo:hi].rearrange("p j (c i) -> p c j i", i=4),
+    )
+
+
+def tile_mix_glu48_fm_pl_none_kernel(tc, x, w4_words, w4_scales, w8_words, w8_scales, out_0, out_1, out_2):
+    nc = tc.nc
+    with ExitStack() as ctx:
+        keep = ctx.enter_context(tc.tile_pool(name="keep", bufs=1))
+        gate_pool = ctx.enter_context(tc.tile_pool(name="gate", bufs=6))
+        res_pool = ctx.enter_context(tc.tile_pool(name="res", bufs=4))
+        rounded_pool = ctx.enter_context(tc.tile_pool(name="rounded", bufs=3))
+        code_pool = ctx.enter_context(tc.tile_pool(name="codes", bufs=4))
+        g_psum = ctx.enter_context(tc.psum_pool(name="g_psum", bufs=3))
+        u_psum = ctx.enter_context(tc.psum_pool(name="u_psum", bufs=5))
+        ctx.enter_context(tc.manual_schedule())
+
+        x_raw = [keep.tile([P, PACK, w], F32, name="x_raw%d" % c, align_bytes=64) for c, (t0, w) in enumerate(X_CHUNKS)]
+        w4_raw = [keep.tile([P, 2 * GROUP], U8, name="w4_raw%d" % a, align_bytes=64) for a in range(2)]
+        w8_raw = [keep.tile([P, GROUP], U32, name="w8_raw%d" % a, align_bytes=64) for a in range(2)]
+        w4_dealt = [keep.tile([P, 2 * GROUP], U8, name="w4_dealt%d" % a, align_bytes=64) for a in range(2)]
+        w8_dealt = [keep.tile([P, GROUP], U32, name="w8_dealt%d" % a, align_bytes=64) for a in range(2)]
+        ws_raw = keep.tile([P, 4, M], U8, name="ws_raw", align_bytes=64)
+        ws_dealt = [keep.tile([P, GROUP], U8, name="ws_dealt%d" % a, align_bytes=64) for a in range(2)]
+        x_codes = keep.tile([P, T], U32, name="x_codes", align_bytes=64)
+        x_scales = keep.tile([P, T], U8, name="x_scales", align_bytes=64)
+        out_scales = [keep.tile([P, T], U8, name="out_scales%d" % a, align_bytes=64) for a in range(2)]
+
+        w8_flat = w8_words[0].rearrange("p n i -> p (n i)")
+
+        def load_x(c):
+            t0, w = X_CHUNKS[c]
+            nc.sync.dma_start(out=x_raw[c][:], in_=x[:, t0 : t0 + w].rearrange("(p j) t -> p j t", j=PACK))
+
+        def load_weights(a):
+            nc.sync.dma_start(out=w4_raw[a][:].bitcast(I32), in_=w4_words[0][:, 2 * GROUP * a : 2 * GROUP * (a + 1)].bitcast(I32))
+            nc.sync.dma_start(out=w8_raw[a][:].bitcast(I32), in_=w8_flat[:, 4 * GROUP * a : 4 * GROUP * (a + 1)].bitcast(I32))
+
+        nc.vector.memset(ws_raw[0:QUAD].bitcast(I32), 0)
+        load_x(0)
+        for row, scales in ((0, w4_scales), (W8_ROW, w8_scales)):
+            nc.sync.dma_start(
+                out=ws_raw[row : row + 4].bitcast(I32),
+                in_=scales[0].bitcast(I32).rearrange("(q r) n -> r q n", r=4),
+            )
+        load_weights(0)
+        load_x(1)
+        load_weights(1)
+        load_x(2)
+        load_x(3)
+
+        def deal_scales(a):
+            deal(nc.vector.tensor_copy, ws_dealt[a][:], ws_raw[:, 0, GROUP * a : GROUP * (a + 1)], 16)
+
+        def deal_w4(copy, a):
+            deal(copy, w4_dealt[a][:].bitcast(U16), w4_raw[a][:].bitcast(U16), 8)
+
+        def deal_w8(copy, dtype, a):
+            deal(copy, w8_dealt[a][:].bitcast(dtype), w8_raw[a][:].bitcast(dtype), 4)
+
+        def round_shared(src, w, split):
+            rounded = rounded_pool.tile([P, w, PACK], BF16, name="rounded", align_bytes=64)
+            round_columns(nc.vector.tensor_copy, rounded, src, 0, split)
+            if split < w:
+                round_columns(nc.scalar.copy, rounded, src, split, w)
+            return rounded
+
+        def quantize_x(c, rounded):
+            t0, w = X_CHUNKS[c]
+            nc.vector.quantize_mx(
+                out=x_codes[:, t0 : t0 + w].bitcast(FP8X4),
+                scales=x_scales[:, t0 : t0 + w],
+                in_=rounded[:].rearrange("p t j -> p (t j)"),
+            )
+
+        def quantize_out(unit, rounded):
+            a, t0, w = unit
+            codes = code_pool.tile([P, w], U32, name="codes", align_bytes=64)
+            nc.vector.quantize_mx(
+                out=codes[:].bitcast(FP8X4),
+                scales=out_scales[a][:, t0 : t0 + w],
+                in_=rounded[:].rearrange("p t j -> p (t j)"),
+            )
+            nc.sync.dma_start(
+                out=out_1[a].rearrange("p t i -> p (t i)")[:, 4 * t0 : 4 * (t0 + w)].bitcast(I32),
+                in_=codes[:].bitcast(I32),
+            )
+            if t0 + w == T:
+                for q in range(4):
+                    nc.sync.dma_start(
+                        out=out_2[a, 4 * q : 4 * q + 4, :].bitcast(I32),
+                        in_=out_scales[a][QUAD * q : QUAD * q + 4, :].bitcast(I32),
+                    )
+
+        def gate(unit, r):
+            a, t0, w = unit
+            g = g_psum.tile([P, w], F32, name="g")
+            nc.tensor.matmul_mx(
+                out=g[:],
+                lhsT=w4_dealt[a][:, 2 * P * r : 2 * P * (r + 1)].bitcast(FP4X4),
+                lhsT_scale=ws_dealt[a][:, P * r : P * (r + 1)],
+                rhs=x_codes[:, t0 : t0 + w].bitcast(FP8X4),
+                rhs_scale=x_scales[:, t0 : t0 + w],
+                start=True,
+                stop=True,
+            )
+            act = gate_pool.tile([P, w], F32, name="act", align_bytes=64)
+            nc.scalar.activation(out=act[:], in_=g[:], func=SILU)
+            return act
+
+        def up(unit, r):
+            a, t0, w = unit
+            u = u_psum.tile([P, w], F32, name="u")
+            nc.tensor.matmul_mx(
+                out=u[:],
+                lhsT=w8_dealt[a][:, P * r : P * (r + 1)].bitcast(FP8X4),
+                lhsT_scale=ws_dealt[a][W8_ROW:P, P * r : P * (r + 1)],
+                rhs=x_codes[:, t0 : t0 + w].bitcast(FP8X4),
+                rhs_scale=x_scales[:, t0 : t0 + w],
+                start=True,
+                stop=True,
+            )
+            return u
+
+        rounded_x = round_shared(x_raw[0], X_CHUNKS[0][1], X_CHUNKS[0][1])
+        for q in range(1, 4):
+            nc.vector.tensor_copy(out=ws_raw[QUAD * q : QUAD * (q + 1), 0, :].bitcast(I32), in_=ws_raw[0:QUAD, q, :].bitcast(I32))
+        quantize_x(0, rounded_x)
+        deal_scales(0)
+        deal_w4(nc.vector.tensor_copy, 0)
+        deal_w8(nc.vector.tensor_copy, I32, 0)
+
+        steps = [(unit, r) for unit in UNITS for r in range(PACK)]
+        act = gate(*steps[0])
+        chunk_of = dict((t0, c) for c, (t0, w) in enumerate(X_CHUNKS))
+        prepared = set([0])
+        prev = None
+        for n, unit in enumerate(UNITS):
+            a, t0, w = unit
+            nxt = UNITS[n + 1] if n + 1 < len(UNITS) else None
+            chunk = chunk_of.get(nxt[1]) if nxt else None
+            if chunk in prepared:
+                chunk = None
+            res = res_pool.tile([P, PACK, w], F32, name="res", align_bytes=64)
+            rows = out_0[GROUP * a : GROUP * (a + 1), t0 : t0 + w].rearrange("(p j) t -> p j t", j=PACK)
+            for r in range(PACK):
+                u = up(unit, r)
+                s = PACK * n + r + 1
+                next_act = gate(*steps[s]) if s < len(steps) else None
+                nc.vector.tensor_tensor(out=res[:, r, :], in0=u[:], in1=act[:], op=MULT)
+                act = next_act
+                if r % 2 == 1:
+                    nc.sync.dma_start(out=rows[:, r - 1 : r + 1, :], in_=res[:, r - 1 : r + 1, :])
+                if r == 0:
+                    if chunk is not None:
+                        rounded_x = round_shared(x_raw[chunk], X_CHUNKS[chunk][1], X_CHUNKS[chunk][1] // 2)
+                    if n == 1:
+                        deal_w4(nc.scalar.copy, 1)
+                        deal_w8(nc.scalar.copy, U32, 1)
+                        deal_scales(1)
+                if r == 1:
+                    if prev is not None:
+                        rounded_prev = round_shared(prev[1], prev[0][2], prev[0][2] // 2)
+                    if chunk is not None:
+                        quantize_x(chunk, rounded_x)
+                        prepared.add(chunk)
+                if r == 2 and prev is not None:
+                    quantize_out(prev[0], rounded_prev)
+            prev = (unit, res)
+        rounded_prev = round_shared(prev[1], prev[0][2], 160)
+        quantize_out(prev[0], rounded_prev)

@@ -15,25 +15,31 @@ FP8X4 = mybir.dt.float8_e4m3fn_x4
 FP4X4 = mybir.dt.float4_e2m1fn_x4
 SILU = mybir.ActivationFunctionType.Silu
 MULT = mybir.AluOpType.mult
+ADD = mybir.AluOpType.add
 
 P = 128
 PACK = 4
 GROUP = P * PACK
 QUAD = 32
+BANK = 512
+LINE = 16
 W8_ROW = 4
 
 X_CHUNKS = [(0, 256), (256, 256), (512, 512), (1024, 512)]
 UNITS = [(0, 0, 256), (0, 256, 256), (1, 0, 512), (0, 512, 512), (1, 512, 512), (0, 1024, 512), (1, 1024, 256), (1, 1280, 256)]
+GPSIMD_SHARE = (3, 4)
+LAST_VECTOR_COLUMNS = 160
+EARLY_SCALE_COLUMNS = 1024
 
 
 def deal(copy, dst, src, run):
-    copy(out=dst.rearrange("p (r c i) -> p c r i", r=PACK, i=run), in_=src.rearrange("p (c i r) -> p c r i", r=PACK, i=run))
+    copy(out=dst.rearrange("p (j c i) -> p c j i", j=PACK, i=run), in_=src.rearrange("p (c i j) -> p c j i", j=PACK, i=run))
 
 
-def round_columns(copy, dst, src, lo, hi):
+def round_columns(copy, dst, src, lo, hi, run):
     copy(
-        out=dst[:, lo:hi, :].rearrange("p (c i) j -> p c j i", i=4),
-        in_=src[:, :, lo:hi].rearrange("p j (c i) -> p c j i", i=4),
+        out=dst[:, lo:hi, :].rearrange("p (c i) j -> p c j i", i=run),
+        in_=src[:, :, lo:hi].rearrange("p j (c i) -> p c j i", i=run),
     )
 
 
@@ -42,164 +48,185 @@ def tile_mix_glu48_fm_pl_none_kernel(tc, x, w4_words, w4_scales, w8_words, w8_sc
     with ExitStack() as ctx:
         keep = ctx.enter_context(tc.tile_pool(name="keep", bufs=1))
         gate_pool = ctx.enter_context(tc.tile_pool(name="gate", bufs=6))
-        res_pool = ctx.enter_context(tc.tile_pool(name="res", bufs=4))
-        rounded_pool = ctx.enter_context(tc.tile_pool(name="rounded", bufs=3))
+        result_pool = ctx.enter_context(tc.tile_pool(name="result", bufs=4))
         code_pool = ctx.enter_context(tc.tile_pool(name="codes", bufs=4))
         g_psum = ctx.enter_context(tc.psum_pool(name="g_psum", bufs=3))
         u_psum = ctx.enter_context(tc.psum_pool(name="u_psum", bufs=5))
         ctx.enter_context(tc.manual_schedule())
 
         x_raw = [keep.tile([P, PACK, w], F32, name="x_raw%d" % c, align_bytes=64) for c, (t0, w) in enumerate(X_CHUNKS)]
+        x_rounded = [keep.tile([P, w, PACK], BF16, name="x_rounded%d" % c, align_bytes=64) for c, (t0, w) in enumerate(X_CHUNKS)]
+        x_codes = keep.tile([P, T], U32, name="x_codes", align_bytes=64)
+        x_scales = keep.tile([P, T], U8, name="x_scales", align_bytes=64)
         w4_raw = [keep.tile([P, 2 * GROUP], U8, name="w4_raw%d" % a, align_bytes=64) for a in range(2)]
         w8_raw = [keep.tile([P, GROUP], U32, name="w8_raw%d" % a, align_bytes=64) for a in range(2)]
         w4_dealt = [keep.tile([P, 2 * GROUP], U8, name="w4_dealt%d" % a, align_bytes=64) for a in range(2)]
         w8_dealt = [keep.tile([P, GROUP], U32, name="w8_dealt%d" % a, align_bytes=64) for a in range(2)]
-        ws_raw = keep.tile([P, 4, M], U8, name="ws_raw", align_bytes=64)
+        ws_landed = keep.tile([2 * W8_ROW, 4, M], U8, name="ws_landed", align_bytes=64)
+        ws_spread = keep.tile([P, 2, M], U8, name="ws_spread", align_bytes=64)
         ws_dealt = [keep.tile([P, GROUP], U8, name="ws_dealt%d" % a, align_bytes=64) for a in range(2)]
-        x_codes = keep.tile([P, T], U32, name="x_codes", align_bytes=64)
-        x_scales = keep.tile([P, T], U8, name="x_scales", align_bytes=64)
-        out_scales = [keep.tile([P, T], U8, name="out_scales%d" % a, align_bytes=64) for a in range(2)]
-
-        w8_flat = w8_words[0].rearrange("p n i -> p (n i)")
+        out_scales = keep.tile([P, 2, T], U8, name="out_scales", align_bytes=64)
 
         def load_x(c):
             t0, w = X_CHUNKS[c]
             nc.sync.dma_start(out=x_raw[c][:], in_=x[:, t0 : t0 + w].rearrange("(p j) t -> p j t", j=PACK))
 
         def load_weights(a):
+            w8_flat = w8_words[0].rearrange("p n i -> p (n i)")
             nc.sync.dma_start(out=w4_raw[a][:].bitcast(I32), in_=w4_words[0][:, 2 * GROUP * a : 2 * GROUP * (a + 1)].bitcast(I32))
             nc.sync.dma_start(out=w8_raw[a][:].bitcast(I32), in_=w8_flat[:, 4 * GROUP * a : 4 * GROUP * (a + 1)].bitcast(I32))
 
-        nc.vector.memset(ws_raw[0:QUAD].bitcast(I32), 0)
-        load_x(0)
+        def deal_scales(a):
+            deal(nc.vector.tensor_copy, ws_dealt[a][:], ws_spread[:, 0, GROUP * a : GROUP * (a + 1)], LINE)
+
+        def deal_w4(copy, a):
+            deal(copy, w4_dealt[a][:].bitcast(U16), w4_raw[a][:].bitcast(U16), LINE // 2)
+
+        def deal_w8(copy, dtype, a):
+            deal(copy, w8_dealt[a][:].bitcast(dtype), w8_raw[a][:].bitcast(dtype), LINE // 4)
+
+        def round_on_vector(dst, src, lo, hi):
+            round_columns(nc.vector.tensor_copy, dst, src, lo, hi, 2)
+
+        def round_on_scalar(dst, src, lo, hi):
+            round_columns(nc.scalar.copy, dst, src, lo, hi, 2)
+
+        def round_on_gpsimd(dst, src, lo, hi):
+            def identity(out, in_):
+                nc.gpsimd.tensor_scalar(out=out, in0=in_, scalar1=1.0, scalar2=-0.0, op0=MULT, op1=ADD)
+
+            round_columns(identity, dst, src, lo, hi, 1)
+
+        def quantize_x(c):
+            t0, w = X_CHUNKS[c]
+            nc.vector.quantize_mx(
+                out=x_codes[:, t0 : t0 + w].bitcast(FP8X4),
+                scales=x_scales[:, t0 : t0 + w],
+                in_=x_rounded[c][:].rearrange("p t j -> p (t j)"),
+            )
+
+        def quantize_result(n, rounded):
+            a, t0, w = UNITS[n]
+            codes = code_pool.tile([P, w], U32, name="codes", align_bytes=64)
+            nc.vector.quantize_mx(
+                out=codes[:].bitcast(FP8X4),
+                scales=out_scales[:, a, t0 : t0 + w],
+                in_=rounded[:].rearrange("p t j -> p (t j)"),
+            )
+            nc.sync.dma_start(
+                out=out_1[a].rearrange("p t i -> p (t i)")[:, PACK * t0 : PACK * (t0 + w)].bitcast(I32),
+                in_=codes[:].bitcast(I32),
+            )
+
+        def store_scales(lo, hi, queues):
+            for q in range(4):
+                queues[q % len(queues)].dma_start(
+                    out=out_2[:, 4 * q : 4 * q + 4, lo:hi].rearrange("a r t -> r a t").bitcast(I32),
+                    in_=out_scales[QUAD * q : QUAD * q + 4, :, lo:hi].bitcast(I32),
+                )
+
+        def product(bank, n, step, dealt, slot_width, dtype, scale_row):
+            a, t0, w = UNITS[n]
+            slots = BANK // w
+            for i in range(slots):
+                j = step * slots + i
+                nc.tensor.matmul_mx(
+                    out=bank[:, i * w : (i + 1) * w],
+                    lhsT=dealt[a][:, slot_width * j : slot_width * (j + 1)].bitcast(dtype),
+                    lhsT_scale=ws_dealt[a][scale_row:P, P * j : P * (j + 1)],
+                    rhs=x_codes[:, t0 : t0 + w].bitcast(FP8X4),
+                    rhs_scale=x_scales[:, t0 : t0 + w],
+                    start=True,
+                    stop=True,
+                )
+
+        def gate(n, step):
+            g = g_psum.tile([P, BANK], F32, name="g")
+            product(g, n, step, w4_dealt, 2 * P, FP4X4, 0)
+            act = gate_pool.tile([P, BANK], F32, name="act", align_bytes=64)
+            nc.scalar.activation(out=act[:], in_=g[:], func=SILU)
+            return act
+
+        def up(n, step):
+            u = u_psum.tile([P, BANK], F32, name="u")
+            product(u, n, step, w8_dealt, P, FP8X4, W8_ROW)
+            return u
+
         for row, scales in ((0, w4_scales), (W8_ROW, w8_scales)):
             nc.sync.dma_start(
-                out=ws_raw[row : row + 4].bitcast(I32),
+                out=ws_landed[row : row + 4].bitcast(I32),
                 in_=scales[0].bitcast(I32).rearrange("(q r) n -> r q n", r=4),
             )
+        load_x(0)
         load_weights(0)
         load_x(1)
         load_weights(1)
         load_x(2)
         load_x(3)
 
-        def deal_scales(a):
-            deal(nc.vector.tensor_copy, ws_dealt[a][:], ws_raw[:, 0, GROUP * a : GROUP * (a + 1)], 16)
-
-        def deal_w4(copy, a):
-            deal(copy, w4_dealt[a][:].bitcast(U16), w4_raw[a][:].bitcast(U16), 8)
-
-        def deal_w8(copy, dtype, a):
-            deal(copy, w8_dealt[a][:].bitcast(dtype), w8_raw[a][:].bitcast(dtype), 4)
-
-        def round_shared(src, w, split):
-            rounded = rounded_pool.tile([P, w, PACK], BF16, name="rounded", align_bytes=64)
-            round_columns(nc.vector.tensor_copy, rounded, src, 0, split)
-            if split < w:
-                round_columns(nc.scalar.copy, rounded, src, split, w)
-            return rounded
-
-        def quantize_x(c, rounded):
-            t0, w = X_CHUNKS[c]
-            nc.vector.quantize_mx(
-                out=x_codes[:, t0 : t0 + w].bitcast(FP8X4),
-                scales=x_scales[:, t0 : t0 + w],
-                in_=rounded[:].rearrange("p t j -> p (t j)"),
-            )
-
-        def quantize_out(unit, rounded):
-            a, t0, w = unit
-            codes = code_pool.tile([P, w], U32, name="codes", align_bytes=64)
-            nc.vector.quantize_mx(
-                out=codes[:].bitcast(FP8X4),
-                scales=out_scales[a][:, t0 : t0 + w],
-                in_=rounded[:].rearrange("p t j -> p (t j)"),
-            )
-            nc.sync.dma_start(
-                out=out_1[a].rearrange("p t i -> p (t i)")[:, 4 * t0 : 4 * (t0 + w)].bitcast(I32),
-                in_=codes[:].bitcast(I32),
-            )
-            if t0 + w == T:
-                for q in range(4):
-                    nc.sync.dma_start(
-                        out=out_2[a, 4 * q : 4 * q + 4, :].bitcast(I32),
-                        in_=out_scales[a][QUAD * q : QUAD * q + 4, :].bitcast(I32),
-                    )
-
-        def gate(unit, r):
-            a, t0, w = unit
-            g = g_psum.tile([P, w], F32, name="g")
-            nc.tensor.matmul_mx(
-                out=g[:],
-                lhsT=w4_dealt[a][:, 2 * P * r : 2 * P * (r + 1)].bitcast(FP4X4),
-                lhsT_scale=ws_dealt[a][:, P * r : P * (r + 1)],
-                rhs=x_codes[:, t0 : t0 + w].bitcast(FP8X4),
-                rhs_scale=x_scales[:, t0 : t0 + w],
-                start=True,
-                stop=True,
-            )
-            act = gate_pool.tile([P, w], F32, name="act", align_bytes=64)
-            nc.scalar.activation(out=act[:], in_=g[:], func=SILU)
-            return act
-
-        def up(unit, r):
-            a, t0, w = unit
-            u = u_psum.tile([P, w], F32, name="u")
-            nc.tensor.matmul_mx(
-                out=u[:],
-                lhsT=w8_dealt[a][:, P * r : P * (r + 1)].bitcast(FP8X4),
-                lhsT_scale=ws_dealt[a][W8_ROW:P, P * r : P * (r + 1)],
-                rhs=x_codes[:, t0 : t0 + w].bitcast(FP8X4),
-                rhs_scale=x_scales[:, t0 : t0 + w],
-                start=True,
-                stop=True,
-            )
-            return u
-
-        rounded_x = round_shared(x_raw[0], X_CHUNKS[0][1], X_CHUNKS[0][1])
-        for q in range(1, 4):
-            nc.vector.tensor_copy(out=ws_raw[QUAD * q : QUAD * (q + 1), 0, :].bitcast(I32), in_=ws_raw[0:QUAD, q, :].bitcast(I32))
-        quantize_x(0, rounded_x)
+        nc.vector.memset(ws_spread[:].bitcast(I32), 0)
+        for q in range(4):
+            first = QUAD * (q % 2)
+            nc.vector.tensor_copy(out=ws_spread[first : first + 2 * W8_ROW, q // 2, :].bitcast(I32), in_=ws_landed[:, q, :].bitcast(I32))
+        nc.vector.tensor_copy(out=ws_spread[2 * QUAD : P, 0, :].bitcast(I32), in_=ws_spread[0 : 2 * QUAD, 1, :].bitcast(I32))
+        round_on_vector(x_rounded[0], x_raw[0], 0, X_CHUNKS[0][1])
         deal_scales(0)
+        quantize_x(0)
         deal_w4(nc.vector.tensor_copy, 0)
         deal_w8(nc.vector.tensor_copy, I32, 0)
+        round_on_gpsimd(x_rounded[1], x_raw[1], 0, X_CHUNKS[1][1])
 
-        steps = [(unit, r) for unit in UNITS for r in range(PACK)]
+        steps = [(n, s) for n, unit in enumerate(UNITS) for s in range(unit[2] * PACK // BANK)]
+        last = len(UNITS) - 1
+        results = {}
+        rounded = {}
+        scalar_rest = {}
         act = gate(*steps[0])
-        chunk_of = dict((t0, c) for c, (t0, w) in enumerate(X_CHUNKS))
-        prepared = set([0])
-        prev = None
-        for n, unit in enumerate(UNITS):
-            a, t0, w = unit
-            nxt = UNITS[n + 1] if n + 1 < len(UNITS) else None
-            chunk = chunk_of.get(nxt[1]) if nxt else None
-            if chunk in prepared:
-                chunk = None
-            res = res_pool.tile([P, PACK, w], F32, name="res", align_bytes=64)
-            rows = out_0[GROUP * a : GROUP * (a + 1), t0 : t0 + w].rearrange("(p j) t -> p j t", j=PACK)
-            for r in range(PACK):
-                u = up(unit, r)
-                s = PACK * n + r + 1
-                next_act = gate(*steps[s]) if s < len(steps) else None
-                nc.vector.tensor_tensor(out=res[:, r, :], in0=u[:], in1=act[:], op=MULT)
-                act = next_act
-                if r % 2 == 1:
-                    nc.sync.dma_start(out=rows[:, r - 1 : r + 1, :], in_=res[:, r - 1 : r + 1, :])
-                if r == 0:
-                    if chunk is not None:
-                        rounded_x = round_shared(x_raw[chunk], X_CHUNKS[chunk][1], X_CHUNKS[chunk][1] // 2)
-                    if n == 1:
-                        deal_w4(nc.scalar.copy, 1)
-                        deal_w8(nc.scalar.copy, U32, 1)
-                        deal_scales(1)
-                if r == 1:
-                    if prev is not None:
-                        rounded_prev = round_shared(prev[1], prev[0][2], prev[0][2] // 2)
-                    if chunk is not None:
-                        quantize_x(chunk, rounded_x)
-                        prepared.add(chunk)
-                if r == 2 and prev is not None:
-                    quantize_out(prev[0], rounded_prev)
-            prev = (unit, res)
-        rounded_prev = round_shared(prev[1], prev[0][2], 160)
-        quantize_out(prev[0], rounded_prev)
+        for k, (n, s) in enumerate(steps):
+            a, t0, w = UNITS[n]
+            slots = BANK // w
+            lo, hi = s * slots, (s + 1) * slots
+            unit_done = hi == PACK
+            if s == 0:
+                results[n] = result_pool.tile([P, PACK, w], F32, name="result", align_bytes=64)
+            u = up(n, s)
+            next_act = gate(*steps[k + 1]) if k + 1 < len(steps) else None
+            nc.vector.tensor_tensor(out=results[n][:, lo:hi, :].rearrange("p j t -> p (j t)"), in0=u[:], in1=act[:], op=MULT)
+            act = next_act
+
+            per_store = 1 if n == last else 2
+            if s % per_store == per_store - 1:
+                first = hi - per_store * slots
+                rows = out_0[GROUP * a : GROUP * (a + 1), t0 : t0 + w].rearrange("(p j) t -> p j t", j=PACK)
+                nc.sync.dma_start(out=rows[:, first:hi, :], in_=results[n][:, first:hi, :])
+
+            if k in scalar_rest:
+                round_on_scalar(*scalar_rest[k])
+            if unit_done and n in (1, 2):
+                round_on_vector(x_rounded[n + 1], x_raw[n + 1], 0, 256)
+            if unit_done and n == last:
+                rounded[n] = keep.tile([P, w, PACK], BF16, name="rounded_last", align_bytes=64)
+                round_on_vector(rounded[n], results[n], 0, LAST_VECTOR_COLUMNS)
+                round_on_scalar(rounded[n], results[n], LAST_VECTOR_COLUMNS, w)
+            if unit_done and n > 0:
+                quantize_result(n - 1, rounded[n - 1])
+            if k in (0, 5, 7):
+                quantize_x({0: 1, 5: 2, 7: 3}[k])
+            if unit_done and n < last:
+                rounded[n] = keep.tile([P, w, PACK], BF16, name="rounded", align_bytes=64)
+                split = min(w, UNITS[n + 1][2] * GPSIMD_SHARE[0] // GPSIMD_SHARE[1])
+                round_on_gpsimd(rounded[n], results[n], 0, split)
+                if split < w:
+                    scalar_rest[k + 2] = (rounded[n], results[n], split, w)
+            if unit_done and n > 0 and UNITS[n - 1] == (1, 512, 512):
+                store_scales(0, EARLY_SCALE_COLUMNS, [nc.sync])
+            if k == 0:
+                deal_w4(nc.scalar.copy, 1)
+            if k == 1:
+                deal_scales(1)
+                deal_w8(nc.scalar.copy, U32, 1)
+            if 3 <= k <= 6:
+                c, quarter = divmod(k + 1, 2)
+                round_on_scalar(x_rounded[c], x_raw[c], 256 + 128 * quarter, 384 + 128 * quarter)
+        quantize_result(last, rounded[last])
+        store_scales(EARLY_SCALE_COLUMNS, T, [nc.scalar, nc.sync])

@@ -26,9 +26,14 @@ LINE = 16
 W8_ROW = 4
 
 X_CHUNKS = [(0, 256), (256, 256), (512, 512), (1024, 512)]
-UNITS = [(0, 0, 256), (0, 256, 256), (1, 0, 512), (0, 512, 512), (1, 512, 512), (0, 1024, 512), (1, 1024, 256), (1, 1280, 256)]
-GPSIMD_SHARE = (3, 4)
-LAST_VECTOR_COLUMNS = 160
+UNITS = [(0, 0, 256), (0, 256, 256), (1, 0, 512), (0, 512, 512), (1, 512, 512), (0, 1024, 512), (1, 1024, 512)]
+BLOCK = 512
+GPSIMD_SIXTEENTHS = 11
+SCALAR_DELAY = 3
+FIRST_VECTOR_COLUMNS = 128
+LAST_VECTOR_COLUMNS = 320
+X_VECTOR_COLUMNS = {2: 384, 3: 128}
+X_PIECE = 128
 EARLY_SCALE_COLUMNS = 1024
 
 
@@ -79,11 +84,11 @@ def tile_mix_glu48_fm_pl_none_kernel(tc, x, w4_words, w4_scales, w8_words, w8_sc
         def deal_scales(a):
             deal(nc.vector.tensor_copy, ws_dealt[a][:], ws_spread[:, 0, GROUP * a : GROUP * (a + 1)], LINE)
 
-        def deal_w4(copy, a):
-            deal(copy, w4_dealt[a][:].bitcast(U16), w4_raw[a][:].bitcast(U16), LINE // 2)
+        def deal_w4(a):
+            deal(nc.scalar.copy, w4_dealt[a][:].bitcast(U16), w4_raw[a][:].bitcast(U16), LINE // 2)
 
-        def deal_w8(copy, dtype, a):
-            deal(copy, w8_dealt[a][:].bitcast(dtype), w8_raw[a][:].bitcast(dtype), LINE // 4)
+        def deal_w8(a):
+            deal(nc.vector.tensor_copy, w8_dealt[a][:].bitcast(I32), w8_raw[a][:].bitcast(I32), LINE // 4)
 
         def round_on_vector(dst, src, lo, hi):
             round_columns(nc.vector.tensor_copy, dst, src, lo, hi, 2)
@@ -105,24 +110,29 @@ def tile_mix_glu48_fm_pl_none_kernel(tc, x, w4_words, w4_scales, w8_words, w8_sc
                 in_=x_rounded[c][:].rearrange("p t j -> p (t j)"),
             )
 
+        codes = {}
+
         def quantize_result(n, rounded):
             a, t0, w = UNITS[n]
-            codes = code_pool.tile([P, w], U32, name="codes", align_bytes=64)
+            b, lo = divmod(t0, BLOCK)
+            if lo == 0:
+                codes[a, b] = code_pool.tile([P, BLOCK], U32, name="codes", align_bytes=64)
             nc.vector.quantize_mx(
-                out=codes[:].bitcast(FP8X4),
+                out=codes[a, b][:, lo : lo + w].bitcast(FP8X4),
                 scales=out_scales[:, a, t0 : t0 + w],
                 in_=rounded[:].rearrange("p t j -> p (t j)"),
             )
-            nc.sync.dma_start(
-                out=out_1[a].rearrange("p t i -> p (t i)")[:, PACK * t0 : PACK * (t0 + w)].bitcast(I32),
-                in_=codes[:].bitcast(I32),
-            )
+            if lo + w == BLOCK:
+                nc.sync.dma_start(
+                    out=out_1[a].rearrange("p t i -> p (t i)")[:, PACK * BLOCK * b : PACK * BLOCK * (b + 1)].bitcast(I32),
+                    in_=codes[a, b][:].bitcast(I32),
+                )
 
         def store_scales(lo, hi, queues):
-            for q in range(4):
-                queues[q % len(queues)].dma_start(
-                    out=out_2[:, 4 * q : 4 * q + 4, lo:hi].rearrange("a r t -> r a t").bitcast(I32),
-                    in_=out_scales[QUAD * q : QUAD * q + 4, :, lo:hi].bitcast(I32),
+            for r in range(4):
+                queues[r % len(queues)].dma_start(
+                    out=out_2[:, r:16:4, lo:hi].rearrange("a q t -> q a t").bitcast(I32),
+                    in_=out_scales[r:P:QUAD, :, lo:hi].bitcast(I32),
                 )
 
         def product(bank, n, step, dealt, slot_width, dtype, scale_row):
@@ -152,8 +162,8 @@ def tile_mix_glu48_fm_pl_none_kernel(tc, x, w4_words, w4_scales, w8_words, w8_sc
             product(u, n, step, w8_dealt, P, FP8X4, W8_ROW)
             return u
 
-        for row, scales in ((0, w4_scales), (W8_ROW, w8_scales)):
-            nc.sync.dma_start(
+        for queue, row, scales in ((nc.sync, 0, w4_scales), (nc.scalar, W8_ROW, w8_scales)):
+            queue.dma_start(
                 out=ws_landed[row : row + 4].bitcast(I32),
                 in_=scales[0].bitcast(I32).rearrange("(q r) n -> r q n", r=4),
             )
@@ -164,69 +174,88 @@ def tile_mix_glu48_fm_pl_none_kernel(tc, x, w4_words, w4_scales, w8_words, w8_sc
         load_x(2)
         load_x(3)
 
+        warm = keep.tile([P, 2], F32, name="warm")
+        nc.gpsimd.memset(warm[:, 0:1], 0.0)
+        nc.scalar.activation(out=warm[:, 1:2], in_=warm[:, 0:1], func=SILU)
+
         nc.vector.memset(ws_spread[:].bitcast(I32), 0)
         for q in range(4):
             first = QUAD * (q % 2)
             nc.vector.tensor_copy(out=ws_spread[first : first + 2 * W8_ROW, q // 2, :].bitcast(I32), in_=ws_landed[:, q, :].bitcast(I32))
         nc.vector.tensor_copy(out=ws_spread[2 * QUAD : P, 0, :].bitcast(I32), in_=ws_spread[0 : 2 * QUAD, 1, :].bitcast(I32))
-        round_on_vector(x_rounded[0], x_raw[0], 0, X_CHUNKS[0][1])
+        round_on_vector(x_rounded[0], x_raw[0], 0, FIRST_VECTOR_COLUMNS)
+        round_on_scalar(x_rounded[0], x_raw[0], FIRST_VECTOR_COLUMNS, X_CHUNKS[0][1])
         deal_scales(0)
+        deal_w4(0)
         quantize_x(0)
-        deal_w4(nc.vector.tensor_copy, 0)
-        deal_w8(nc.vector.tensor_copy, I32, 0)
-        round_on_gpsimd(x_rounded[1], x_raw[1], 0, X_CHUNKS[1][1])
+        deal_w8(0)
+        round_on_vector(x_rounded[1], x_raw[1], 0, X_CHUNKS[1][1])
 
         steps = [(n, s) for n, unit in enumerate(UNITS) for s in range(unit[2] * PACK // BANK)]
+        last_step = dict((n, k) for k, (n, s) in enumerate(steps))
         last = len(UNITS) - 1
-        results = {}
+
+        x_due = {}
+        scalar_work = {}
+        for c in X_VECTOR_COLUMNS:
+            first_reader = min(n for n, unit in enumerate(UNITS) if unit[1] == X_CHUNKS[c][0])
+            k = last_step[first_reader - 2]
+            x_due[k] = c
+            pieces = list(range(X_VECTOR_COLUMNS[c], X_CHUNKS[c][1], X_PIECE))
+            for i, lo in enumerate(reversed(pieces)):
+                scalar_work[k - 1 - 2 * i] = [(x_rounded[c], x_raw[c], lo, lo + X_PIECE)]
+
+        blocks = {}
         rounded = {}
-        scalar_rest = {}
         act = gate(*steps[0])
         for k, (n, s) in enumerate(steps):
             a, t0, w = UNITS[n]
+            b, col = divmod(t0, BLOCK)
             slots = BANK // w
             lo, hi = s * slots, (s + 1) * slots
-            unit_done = hi == PACK
-            if s == 0:
-                results[n] = result_pool.tile([P, PACK, w], F32, name="result", align_bytes=64)
+            if s == 0 and col == 0:
+                blocks[a, b] = result_pool.tile([P, PACK, BLOCK], F32, name="result", align_bytes=64)
+            result = blocks[a, b][:, :, col : col + w]
             u = up(n, s)
             next_act = gate(*steps[k + 1]) if k + 1 < len(steps) else None
-            nc.vector.tensor_tensor(out=results[n][:, lo:hi, :].rearrange("p j t -> p (j t)"), in0=u[:], in1=act[:], op=MULT)
+            nc.vector.tensor_tensor(
+                out=result[:, lo:hi, :],
+                in0=u[:].rearrange("p (j t) -> p j t", j=slots),
+                in1=act[:].rearrange("p (j t) -> p j t", j=slots),
+                op=MULT,
+            )
             act = next_act
 
             per_store = 1 if n == last else 2
-            if s % per_store == per_store - 1:
-                first = hi - per_store * slots
-                rows = out_0[GROUP * a : GROUP * (a + 1), t0 : t0 + w].rearrange("(p j) t -> p j t", j=PACK)
-                nc.sync.dma_start(out=rows[:, first:hi, :], in_=results[n][:, first:hi, :])
+            if col + w == BLOCK and hi % per_store == 0:
+                rows = out_0[GROUP * a : GROUP * (a + 1), BLOCK * b : BLOCK * (b + 1)].rearrange("(p j) t -> p j t", j=PACK)
+                nc.sync.dma_start(out=rows[:, hi - per_store : hi, :], in_=blocks[a, b][:, hi - per_store : hi, :])
 
-            if k in scalar_rest:
-                round_on_scalar(*scalar_rest[k])
-            if unit_done and n in (1, 2):
-                round_on_vector(x_rounded[n + 1], x_raw[n + 1], 0, 256)
-            if unit_done and n == last:
+            for work in scalar_work.get(k, []):
+                round_on_scalar(*work)
+            if k in x_due:
+                round_on_vector(x_rounded[x_due[k]], x_raw[x_due[k]], 0, X_VECTOR_COLUMNS[x_due[k]])
+            if k == last_step[last]:
                 rounded[n] = keep.tile([P, w, PACK], BF16, name="rounded_last", align_bytes=64)
-                round_on_vector(rounded[n], results[n], 0, LAST_VECTOR_COLUMNS)
-                round_on_scalar(rounded[n], results[n], LAST_VECTOR_COLUMNS, w)
-            if unit_done and n > 0:
+                round_on_vector(rounded[n], result, 0, LAST_VECTOR_COLUMNS)
+                round_on_scalar(rounded[n], result, LAST_VECTOR_COLUMNS, w)
+            if k == last_step[n] and n > 0:
                 quantize_result(n - 1, rounded[n - 1])
-            if k in (0, 5, 7):
-                quantize_x({0: 1, 5: 2, 7: 3}[k])
-            if unit_done and n < last:
+                if n == last - 1:
+                    store_scales(0, EARLY_SCALE_COLUMNS, [nc.sync])
+            if k in x_due:
+                quantize_x(x_due[k])
+            if k == last_step[n] and n < last:
                 rounded[n] = keep.tile([P, w, PACK], BF16, name="rounded", align_bytes=64)
-                split = min(w, UNITS[n + 1][2] * GPSIMD_SHARE[0] // GPSIMD_SHARE[1])
-                round_on_gpsimd(rounded[n], results[n], 0, split)
+                split = min(w, UNITS[n + 1][2] * GPSIMD_SIXTEENTHS // 16)
+                round_on_gpsimd(rounded[n], result, 0, split)
                 if split < w:
-                    scalar_rest[k + 2] = (rounded[n], results[n], split, w)
-            if unit_done and n > 0 and UNITS[n - 1] == (1, 512, 512):
-                store_scales(0, EARLY_SCALE_COLUMNS, [nc.sync])
+                    scalar_work.setdefault(min(k + SCALAR_DELAY, last_step[n + 1]), []).append((rounded[n], result, split, w))
             if k == 0:
-                deal_w4(nc.scalar.copy, 1)
-            if k == 1:
+                quantize_x(1)
                 deal_scales(1)
-                deal_w8(nc.scalar.copy, U32, 1)
-            if 3 <= k <= 6:
-                c, quarter = divmod(k + 1, 2)
-                round_on_scalar(x_rounded[c], x_raw[c], 256 + 128 * quarter, 384 + 128 * quarter)
+                deal_w4(1)
+            if k == 1:
+                deal_w8(1)
         quantize_result(last, rounded[last])
         store_scales(EARLY_SCALE_COLUMNS, T, [nc.scalar, nc.sync])

@@ -28,7 +28,7 @@ W8_ROW = 4
 X_CHUNKS = [(0, 256), (256, 256), (512, 512), (1024, 512)]
 UNITS = [(0, 0, 256), (0, 256, 256), (1, 0, 512), (0, 512, 512), (1, 512, 512), (0, 1024, 512), (1, 1024, 512)]
 BLOCK = 512
-GPSIMD_SIXTEENTHS = 11
+GPSIMD_COLUMNS = 352
 SCALAR_DELAY = 3
 FIRST_VECTOR_COLUMNS = 128
 LAST_VECTOR_COLUMNS = 320
@@ -189,6 +189,7 @@ def tile_mix_glu48_fm_pl_none_kernel(tc, x, w4_words, w4_scales, w8_words, w8_sc
         deal_w4(0)
         quantize_x(0)
         deal_w8(0)
+        deal_scales(1)
         round_on_vector(x_rounded[1], x_raw[1], 0, X_CHUNKS[1][1])
 
         steps = [(n, s) for n, unit in enumerate(UNITS) for s in range(unit[2] * PACK // BANK)]
@@ -208,6 +209,7 @@ def tile_mix_glu48_fm_pl_none_kernel(tc, x, w4_words, w4_scales, w8_words, w8_sc
         blocks = {}
         rounded = {}
         act = gate(*steps[0])
+        quantize_x(1)
         for k, (n, s) in enumerate(steps):
             a, t0, w = UNITS[n]
             b, col = divmod(t0, BLOCK)
@@ -226,10 +228,9 @@ def tile_mix_glu48_fm_pl_none_kernel(tc, x, w4_words, w4_scales, w8_words, w8_sc
             )
             act = next_act
 
-            per_store = 1 if n == last else 2
-            if col + w == BLOCK and hi % per_store == 0:
+            if col + w == BLOCK:
                 rows = out_0[GROUP * a : GROUP * (a + 1), BLOCK * b : BLOCK * (b + 1)].rearrange("(p j) t -> p j t", j=PACK)
-                nc.sync.dma_start(out=rows[:, hi - per_store : hi, :], in_=blocks[a, b][:, hi - per_store : hi, :])
+                nc.sync.dma_start(out=rows[:, lo:hi, :], in_=blocks[a, b][:, lo:hi, :])
 
             for work in scalar_work.get(k, []):
                 round_on_scalar(*work)
@@ -247,13 +248,11 @@ def tile_mix_glu48_fm_pl_none_kernel(tc, x, w4_words, w4_scales, w8_words, w8_sc
                 quantize_x(x_due[k])
             if k == last_step[n] and n < last:
                 rounded[n] = keep.tile([P, w, PACK], BF16, name="rounded", align_bytes=64)
-                split = min(w, UNITS[n + 1][2] * GPSIMD_SIXTEENTHS // 16)
+                split = min(w, GPSIMD_COLUMNS)
                 round_on_gpsimd(rounded[n], result, 0, split)
                 if split < w:
-                    scalar_work.setdefault(min(k + SCALAR_DELAY, last_step[n + 1]), []).append((rounded[n], result, split, w))
+                    scalar_work.setdefault(k + SCALAR_DELAY, []).append((rounded[n], result, split, w))
             if k == 0:
-                quantize_x(1)
-                deal_scales(1)
                 deal_w4(1)
             if k == 1:
                 deal_w8(1)

from contextlib import ExitStack

import concourse.mybir as mybir

K, M, T = 512, 1024, 1536
FLOPS = 2 * 2 * K * M * T

F32 = mybir.dt.float32
BF16 = mybir.dt.bfloat16
I32 = mybir.dt.int32
U32 = mybir.dt.uint32
U16 = mybir.dt.uint16
U8 = mybir.dt.uint8
FP8X4 = mybir.dt.float8_e4m3fn_x4
FP4X4 = mybir.dt.float4_e2m1fn_x4
SILU = mybir.ActivationFunctionType.Silu
MULT = mybir.AluOpType.mult
ADD = mybir.AluOpType.add

P = 128
PACK = 4
GROUP = P * PACK
QUAD = 32
BANK = 512
LINE = 16
W8_ROW = 4

X_CHUNKS = [(0, 256), (256, 256), (512, 512), (1024, 512)]
UNITS = [(0, 0, 256), (0, 256, 256), (1, 0, 512), (0, 512, 512), (1, 512, 512), (0, 1024, 512), (1, 1024, 512)]
BLOCK = 512
GPSIMD_COLUMNS = 352
SCALAR_DELAY = 3
FIRST_VECTOR_COLUMNS = 128
LAST_VECTOR_COLUMNS = 320
X_VECTOR_COLUMNS = {2: 384, 3: 128}
X_PIECE = 128
EARLY_SCALE_COLUMNS = 1024


def deal(copy, dst, src, run):
    copy(out=dst.rearrange("p (j c i) -> p c j i", j=PACK, i=run), in_=src.rearrange("p (c i j) -> p c j i", j=PACK, i=run))


def round_columns(copy, dst, src, lo, hi, run):
    copy(
        out=dst[:, lo:hi, :].rearrange("p (c i) j -> p c j i", i=run),
        in_=src[:, :, lo:hi].rearrange("p j (c i) -> p c j i", i=run),
    )


def tile_mix_glu48_fm_pl_none_kernel(tc, x, w4_words, w4_scales, w8_words, w8_scales, out_0, out_1, out_2):
    nc = tc.nc
    with ExitStack() as ctx:
        keep = ctx.enter_context(tc.tile_pool(name="keep", bufs=1))
        gate_pool = ctx.enter_context(tc.tile_pool(name="gate", bufs=6))
        result_pool = ctx.enter_context(tc.tile_pool(name="result", bufs=4))
        code_pool = ctx.enter_context(tc.tile_pool(name="codes", bufs=4))
        g_psum = ctx.enter_context(tc.psum_pool(name="g_psum", bufs=3))
        u_psum = ctx.enter_context(tc.psum_pool(name="u_psum", bufs=5))
        ctx.enter_context(tc.manual_schedule())

        x_raw = [keep.tile([P, PACK, w], F32, name="x_raw%d" % c, align_bytes=64) for c, (t0, w) in enumerate(X_CHUNKS)]
        x_rounded = [keep.tile([P, w, PACK], BF16, name="x_rounded%d" % c, align_bytes=64) for c, (t0, w) in enumerate(X_CHUNKS)]
        x_codes = keep.tile([P, T], U32, name="x_codes", align_bytes=64)
        x_scales = keep.tile([P, T], U8, name="x_scales", align_bytes=64)
        w4_raw = [keep.tile([P, 2 * GROUP], U8, name="w4_raw%d" % a, align_bytes=64) for a in range(2)]
        w8_raw = [keep.tile([P, GROUP], U32, name="w8_raw%d" % a, align_bytes=64) for a in range(2)]
        w4_dealt = [keep.tile([P, 2 * GROUP], U8, name="w4_dealt%d" % a, align_bytes=64) for a in range(2)]
        w8_dealt = [keep.tile([P, GROUP], U32, name="w8_dealt%d" % a, align_bytes=64) for a in range(2)]
        ws_landed = keep.tile([2 * W8_ROW, 4, M], U8, name="ws_landed", align_bytes=64)
        ws_spread = keep.tile([P, 2, M], U8, name="ws_spread", align_bytes=64)
        ws_dealt = [keep.tile([P, GROUP], U8, name="ws_dealt%d" % a, align_bytes=64) for a in range(2)]
        out_scales = keep.tile([P, 2, T], U8, name="out_scales", align_bytes=64)

        def load_x(c):
            t0, w = X_CHUNKS[c]
            nc.sync.dma_start(out=x_raw[c][:], in_=x[:, t0 : t0 + w].rearrange("(p j) t -> p j t", j=PACK))

        def load_weights(a):
            w8_flat = w8_words[0].rearrange("p n i -> p (n i)")
            nc.sync.dma_start(out=w4_raw[a][:].bitcast(I32), in_=w4_words[0][:, 2 * GROUP * a : 2 * GROUP * (a + 1)].bitcast(I32))
            nc.sync.dma_start(out=w8_raw[a][:].bitcast(I32), in_=w8_flat[:, 4 * GROUP * a : 4 * GROUP * (a + 1)].bitcast(I32))

        def deal_scales(a):
            deal(nc.vector.tensor_copy, ws_dealt[a][:], ws_spread[:, 0, GROUP * a : GROUP * (a + 1)], LINE)

        def deal_w4(a):
            deal(nc.scalar.copy, w4_dealt[a][:].bitcast(U16), w4_raw[a][:].bitcast(U16), LINE // 2)

        def deal_w8(a):
            deal(nc.vector.tensor_copy, w8_dealt[a][:].bitcast(I32), w8_raw[a][:].bitcast(I32), LINE // 4)

        def round_on_vector(dst, src, lo, hi):
            round_columns(nc.vector.tensor_copy, dst, src, lo, hi, 2)

        def round_on_scalar(dst, src, lo, hi):
            round_columns(nc.scalar.copy, dst, src, lo, hi, 2)

        def round_on_gpsimd(dst, src, lo, hi):
            def identity(out, in_):
                nc.gpsimd.tensor_scalar(out=out, in0=in_, scalar1=1.0, scalar2=-0.0, op0=MULT, op1=ADD)

            round_columns(identity, dst, src, lo, hi, 1)

        def quantize_x(c):
            t0, w = X_CHUNKS[c]
            nc.vector.quantize_mx(
                out=x_codes[:, t0 : t0 + w].bitcast(FP8X4),
                scales=x_scales[:, t0 : t0 + w],
                in_=x_rounded[c][:].rearrange("p t j -> p (t j)"),
            )

        codes = {}

        def quantize_result(n, rounded):
            a, t0, w = UNITS[n]
            b, lo = divmod(t0, BLOCK)
            if lo == 0:
                codes[a, b] = code_pool.tile([P, BLOCK], U32, name="codes", align_bytes=64)
            nc.vector.quantize_mx(
                out=codes[a, b][:, lo : lo + w].bitcast(FP8X4),
                scales=out_scales[:, a, t0 : t0 + w],
                in_=rounded[:].rearrange("p t j -> p (t j)"),
            )
            if lo + w == BLOCK:
                nc.sync.dma_start(
                    out=out_1[a].rearrange("p t i -> p (t i)")[:, PACK * BLOCK * b : PACK * BLOCK * (b + 1)].bitcast(I32),
                    in_=codes[a, b][:].bitcast(I32),
                )

        def store_scales(lo, hi, queues):
            for r in range(4):
                queues[r % len(queues)].dma_start(
                    out=out_2[:, r:16:4, lo:hi].rearrange("a q t -> q a t").bitcast(I32),
                    in_=out_scales[r:P:QUAD, :, lo:hi].bitcast(I32),
                )

        def product(bank, n, step, dealt, slot_width, dtype, scale_row):
            a, t0, w = UNITS[n]
            slots = BANK // w
            for i in range(slots):
                j = step * slots + i
                nc.tensor.matmul_mx(
                    out=bank[:, i * w : (i + 1) * w],
                    lhsT=dealt[a][:, slot_width * j : slot_width * (j + 1)].bitcast(dtype),
                    lhsT_scale=ws_dealt[a][scale_row:P, P * j : P * (j + 1)],
                    rhs=x_codes[:, t0 : t0 + w].bitcast(FP8X4),
                    rhs_scale=x_scales[:, t0 : t0 + w],
                    start=True,
                    stop=True,
                )

        def gate(n, step):
            g = g_psum.tile([P, BANK], F32, name="g")
            product(g, n, step, w4_dealt, 2 * P, FP4X4, 0)
            act = gate_pool.tile([P, BANK], F32, name="act", align_bytes=64)
            nc.scalar.activation(out=act[:], in_=g[:], func=SILU)
            return act

        def up(n, step):
            u = u_psum.tile([P, BANK], F32, name="u")
            product(u, n, step, w8_dealt, P, FP8X4, W8_ROW)
            return u

        for queue, row, scales in ((nc.sync, 0, w4_scales), (nc.scalar, W8_ROW, w8_scales)):
            queue.dma_start(
                out=ws_landed[row : row + 4].bitcast(I32),
                in_=scales[0].bitcast(I32).rearrange("(q r) n -> r q n", r=4),
            )
        load_x(0)
        load_weights(0)
        load_x(1)
        load_weights(1)
        load_x(2)
        load_x(3)

        warm = keep.tile([P, 2], F32, name="warm")
        nc.gpsimd.memset(warm[:, 0:1], 0.0)
        nc.scalar.activation(out=warm[:, 1:2], in_=warm[:, 0:1], func=SILU)

        nc.vector.memset(ws_spread[:].bitcast(I32), 0)
        for q in range(4):
            first = QUAD * (q % 2)
            nc.vector.tensor_copy(out=ws_spread[first : first + 2 * W8_ROW, q // 2, :].bitcast(I32), in_=ws_landed[:, q, :].bitcast(I32))
        nc.vector.tensor_copy(out=ws_spread[2 * QUAD : P, 0, :].bitcast(I32), in_=ws_spread[0 : 2 * QUAD, 1, :].bitcast(I32))
        round_on_vector(x_rounded[0], x_raw[0], 0, FIRST_VECTOR_COLUMNS)
        round_on_scalar(x_rounded[0], x_raw[0], FIRST_VECTOR_COLUMNS, X_CHUNKS[0][1])
        deal_scales(0)
        deal_w4(0)
        quantize_x(0)
        deal_w8(0)
        deal_scales(1)
        round_on_vector(x_rounded[1], x_raw[1], 0, X_CHUNKS[1][1])

        steps = [(n, s) for n, unit in enumerate(UNITS) for s in range(unit[2] * PACK // BANK)]
        last_step = dict((n, k) for k, (n, s) in enumerate(steps))
        last = len(UNITS) - 1

        x_due = {}
        scalar_work = {}
        for c in X_VECTOR_COLUMNS:
            first_reader = min(n for n, unit in enumerate(UNITS) if unit[1] == X_CHUNKS[c][0])
            k = last_step[first_reader - 2]
            x_due[k] = c
            pieces = list(range(X_VECTOR_COLUMNS[c], X_CHUNKS[c][1], X_PIECE))
            for i, lo in enumerate(reversed(pieces)):
                scalar_work[k - 1 - 2 * i] = [(x_rounded[c], x_raw[c], lo, lo + X_PIECE)]

        blocks = {}
        rounded = {}
        act = gate(*steps[0])
        quantize_x(1)
        for k, (n, s) in enumerate(steps):
            a, t0, w = UNITS[n]
            b, col = divmod(t0, BLOCK)
            slots = BANK // w
            lo, hi = s * slots, (s + 1) * slots
            if s == 0 and col == 0:
                blocks[a, b] = result_pool.tile([P, PACK, BLOCK], F32, name="result", align_bytes=64)
            result = blocks[a, b][:, :, col : col + w]
            u = up(n, s)
            next_act = gate(*steps[k + 1]) if k + 1 < len(steps) else None
            nc.vector.tensor_tensor(
                out=result[:, lo:hi, :],
                in0=u[:].rearrange("p (j t) -> p j t", j=slots),
                in1=act[:].rearrange("p (j t) -> p j t", j=slots),
                op=MULT,
            )
            act = next_act

            if col + w == BLOCK:
                rows = out_0[GROUP * a : GROUP * (a + 1), BLOCK * b : BLOCK * (b + 1)].rearrange("(p j) t -> p j t", j=PACK)
                nc.sync.dma_start(out=rows[:, lo:hi, :], in_=blocks[a, b][:, lo:hi, :])

            for work in scalar_work.get(k, []):
                round_on_scalar(*work)
            if k in x_due:
                round_on_vector(x_rounded[x_due[k]], x_raw[x_due[k]], 0, X_VECTOR_COLUMNS[x_due[k]])
            if k == last_step[last]:
                rounded[n] = keep.tile([P, w, PACK], BF16, name="rounded_last", align_bytes=64)
                round_on_vector(rounded[n], result, 0, LAST_VECTOR_COLUMNS)
                round_on_scalar(rounded[n], result, LAST_VECTOR_COLUMNS, w)
            if k == last_step[n] and n > 0:
                quantize_result(n - 1, rounded[n - 1])
                if n == last - 1:
                    store_scales(0, EARLY_SCALE_COLUMNS, [nc.sync])
            if k in x_due:
                quantize_x(x_due[k])
            if k == last_step[n] and n < last:
                rounded[n] = keep.tile([P, w, PACK], BF16, name="rounded", align_bytes=64)
                split = min(w, GPSIMD_COLUMNS)
                round_on_gpsimd(rounded[n], result, 0, split)
                if split < w:
                    scalar_work.setdefault(k + SCALAR_DELAY, []).append((rounded[n], result, split, w))
            if k == 0:
                deal_w4(1)
            if k == 1:
                deal_w8(1)
        quantize_result(last, rounded[last])
        store_scales(EARLY_SCALE_COLUMNS, T, [nc.scalar, nc.sync])
